import numpy as np
import ml_dtypes


def mxq(x, axis, fmt="e4m3"):
    dtype, down = {"e4m3": (ml_dtypes.float8_e4m3fn, 7), "e5m2": (ml_dtypes.float8_e5m2, 14)}[fmt]
    v = np.moveaxis(np.asarray(x, np.float32).astype(ml_dtypes.bfloat16).astype(np.float64), axis, -1)
    blocks = v.reshape(v.shape[:-1] + (-1, 32))
    amax = np.abs(blocks).max(-1, keepdims=True)
    byte = np.maximum(np.where(amax > 0, np.frexp(amax)[1] - 1 + 127, 0) - down, 1)
    scale = np.exp2(byte - 127.0)
    codes = (blocks / scale).astype(np.float32).astype(dtype).astype(np.float64)
    return np.moveaxis((codes * scale).reshape(v.shape), -1, axis)


WIDE = False


def mx_kscale(k):
    if not WIDE:
        return np.ones(k)
    levels = np.array([10, -10, 5, -5, 0])
    if k % 512:
        return np.exp2(np.random.permutation(np.resize(levels, k // 32))).repeat(32)
    a = np.empty((k // 512, 16))
    for p in range(k // 512):
        a[p, :8] = np.random.permutation(np.resize(levels, 8))
        for g in range(8):
            far = levels[np.abs(levels - a[p, g]) >= 10]
            a[p, g + 8] = far[np.random.randint(len(far))]
    return np.exp2(a.ravel()).repeat(32)


def f64(x):
    return np.asarray(x).astype(np.float64)


def striped(idx):
    return np.tile(idx.reshape(-1, 16).T, (8, 1)).astype(np.uint16)


def unstriped(offs):
    return offs[:16].T.reshape(-1).astype(np.int64)


def relu2(v):
    return np.maximum(v, 0.0) ** 2


K, T, D, S, V, R, N = 512, 2048, 5, 1280, 256, 8, 128


def setup_inputs():
    n = np.random.standard_normal
    s = mx_kscale(K)[:, None]
    return {
        "xT": (n((K, T)) * s).astype(np.float32),
        "w": (n((D, K, N)) / np.sqrt(D * K) / s[None]).astype(np.float32),
        "b": (0.3 * n((N, 1))).astype(np.float32),
        "offs": striped(np.concatenate([R * np.arange(V) + np.random.randint(0, R, V) for _ in range(D)])),
    }


def reference(xT, w, b, offs):
    idx = unstriped(offs)
    xq = mxq(f64(xT)[:, idx], 0, "e4m3")
    wq = mxq(f64(w), 1, "e4m3")
    y = sum(wq[d].T @ xq[:, d * V:(d + 1) * V] for d in range(D))
    y = relu2(y + f64(b))
    return y

from contextlib import ExitStack

import concourse.mybir as mybir

K, T, D, S, V, N = 512, 2048, 5, 1280, 256, 128
FLOPS = 2 * N * V * D * K

F32 = mybir.dt.float32
BF16 = mybir.dt.bfloat16
U32 = mybir.dt.uint32
U16 = mybir.dt.uint16
U8 = mybir.dt.uint8
FP8X4 = mybir.dt.float8_e4m3fn_x4
ADD = mybir.AluOpType.add
MAX = mybir.AluOpType.max
SQUARE = mybir.ActivationFunctionType.Square

P = 128
PACK = 4
CHUNKS = [(0, 512, 192), (512, 512, 192), (1024, 512, 192), (1536, 256, 160), (1792, 256, 160)]
W_PARTS = [(0, 2), (2, 4), (4, 5)]
BYTE_PARTS = [(0, 2), (2, 4), (4, 5)]


def tile_picked_deform_lin_relu2_def_e_kernel(tc, xT, w, b, offs, out):
    nc = tc.nc
    with ExitStack() as ctx:
        keep = ctx.enter_context(tc.tile_pool(name="keep", bufs=1))
        psum = ctx.enter_context(tc.psum_pool(name="psum", bufs=1))

        offsets = keep.tile([P, S // 16], U16, name="offsets")
        codes = keep.tile([P, T], U32, name="codes", align_bytes=64)
        scales = keep.tile([P, T], U8, name="scales", align_bytes=64)
        picked_codes = keep.tile([P, S], U32, name="picked_codes", align_bytes=64)
        picked_scales = keep.tile([P, S], U8, name="picked_scales", align_bytes=64)
        w_codes = keep.tile([P, D * N], U32, name="w_codes", align_bytes=64)
        w_scales = keep.tile([P, D * N], U8, name="w_scales", align_bytes=64)
        bias = keep.tile([P, 1], F32, name="bias")
        sums = keep.tile([P, V], F32, name="sums")
        result = keep.tile([P, V], F32, name="result")
        acc = psum.tile([P, V], F32, name="acc")

        nc.gpsimd.memset(scales[:], 0)

        x_raw = []
        for i, (c0, width, on_vector) in enumerate(CHUNKS):
            raw = keep.tile([P, PACK, width], F32, name=f"x_raw{i}")
            nc.sync.dma_start(out=raw[:], in_=xT[:, c0 : c0 + width].rearrange("(p j) c -> p j c", j=PACK))
            x_raw.append(raw)
            if i == 0:
                nc.sync.dma_start(offsets[:], offs)
        w_raw = []
        for i, (d0, d1) in enumerate(W_PARTS):
            raw = keep.tile([P, d1 - d0, PACK, N], F32, name=f"w_raw{i}")
            nc.sync.dma_start(out=raw[:], in_=w[d0:d1].rearrange("d (p j) m -> p d j m", j=PACK))
            w_raw.append(raw)
        nc.sync.dma_start(out=bias[:], in_=b)

        x_grouped = []

        def quantize_chunk(i):
            c0, width, on_vector = CHUNKS[i]
            nc.vector.quantize_mx(
                out=codes[:, c0 : c0 + width].bitcast(FP8X4),
                scales=scales[:, c0 : c0 + width],
                in_=x_grouped[i][:].rearrange("p c j -> p (c j)"),
            )

        for i, (c0, width, a) in enumerate(CHUNKS):
            raw = x_raw[i]
            grouped = keep.tile([P, width, PACK], BF16, name=f"x_grouped{i}", align_bytes=64)
            nc.scalar.copy(out=grouped[:, a:width, :], in_=raw[:, :, a:width].rearrange("p j c -> p c j"))
            nc.vector.tensor_copy(out=grouped[:, 0:a, :], in_=raw[:, :, 0:a].rearrange("p j c -> p c j"))
            x_grouped.append(grouped)
            if i > 0:
                quantize_chunk(i - 1)
        quantize_chunk(len(CHUNKS) - 1)

        w_grouped = []
        for i, (d0, d1) in enumerate(W_PARTS):
            grouped = keep.tile([P, d1 - d0, N, PACK], BF16, name=f"w_grouped{i}", align_bytes=64)
            for d in range(d0, d1):
                nc.scalar.copy(out=grouped[:, d - d0], in_=w_raw[i][:, d - d0].rearrange("p j m -> p m j"))
            w_grouped.append(grouped)

        nc.vector.tensor_copy(out=picked_codes[:], in_=codes[:].indirect(offsets[:]))
        for i, (d0, d1) in enumerate(W_PARTS):
            m_cols = slice(d0 * N, d1 * N)
            nc.vector.quantize_mx(
                out=w_codes[:, m_cols].bitcast(FP8X4),
                scales=w_scales[:, m_cols],
                in_=w_grouped[i][:].rearrange("p d m j -> p (d m j)"),
            )
        for d0, d1 in BYTE_PARTS:
            list_cols = slice(d0 * V // 16, d1 * V // 16)
            nc.vector.tensor_copy(
                out=picked_scales[:, d0 * V : d1 * V], in_=scales[:].indirect(offsets[:, list_cols])
            )
            for d in range(d0, d1):
                m_cols = slice(d * N, (d + 1) * N)
                v_cols = slice(d * V, (d + 1) * V)
                nc.tensor.matmul_mx(
                    out=acc[:],
                    lhsT=w_codes[:, m_cols].bitcast(FP8X4),
                    lhsT_scale=w_scales[:, m_cols],
                    rhs=picked_codes[:, v_cols].bitcast(FP8X4),
                    rhs_scale=picked_scales[:, v_cols],
                    start=(d == 0),
                    stop=(d == D - 1),
                )

        for v0 in range(0, V, V // 2):
            half = slice(v0, v0 + V // 2)
            nc.vector.tensor_scalar(sums[:, half], acc[:, half], bias[:], 0.0, ADD, MAX)
            nc.scalar.activation(result[:, half], sums[:, half], SQUARE)
        nc.scalar.dma_start(out=out, in_=result[:])
